import numpy as np
import ml_dtypes


def mxq(x, axis, fmt="e4m3"):
    dtype, down = {"e4m3": (ml_dtypes.float8_e4m3fn, 7), "e5m2": (ml_dtypes.float8_e5m2, 14)}[fmt]
    v = np.moveaxis(np.asarray(x, np.float32).astype(ml_dtypes.bfloat16).astype(np.float64), axis, -1)
    blocks = v.reshape(v.shape[:-1] + (-1, 32))
    amax = np.abs(blocks).max(-1, keepdims=True)
    byte = np.maximum(np.where(amax > 0, np.frexp(amax)[1] - 1 + 127, 0) - down, 1)
    scale = np.exp2(byte - 127.0)
    codes = (blocks / scale).astype(np.float32).astype(dtype).astype(np.float64)
    return np.moveaxis((codes * scale).reshape(v.shape), -1, axis)


WIDE = False


def mx_kscale(k):
    if not WIDE:
        return np.ones(k)
    levels = np.array([10, -10, 5, -5, 0])
    if k % 512:
        return np.exp2(np.random.permutation(np.resize(levels, k // 32))).repeat(32)
    a = np.empty((k // 512, 16))
    for p in range(k // 512):
        a[p, :8] = np.random.permutation(np.resize(levels, 8))
        for g in range(8):
            far = levels[np.abs(levels - a[p, g]) >= 10]
            a[p, g + 8] = far[np.random.randint(len(far))]
    return np.exp2(a.ravel()).repeat(32)


BF16 = ml_dtypes.bfloat16


def bf(x):
    return np.asarray(x, np.float32).astype(BF16)


def f64(x):
    return np.asarray(x).astype(np.float64)


E2M1 = np.array([0.0, 0.5, 1.0, 1.5, 2.0, 3.0, 4.0, 6.0, -0.0, -0.5, -1.0, -1.5, -2.0, -3.0, -4.0, -6.0])


def pack_weight(w, fmt):
    k, n = w.shape
    w = f64(bf(w)).reshape(k // 32, 32, n)
    amax = np.abs(w).max(1)
    if fmt == "e4m3":
        byte = np.frexp(amax)[1] - 1 + 127 - 7
    else:
        mant, ex = np.frexp(amax / 6.0)
        byte = np.where(mant > 0.5, ex, ex - 1) + 127
    byte = np.clip(np.where(amax > 0, byte, 1), 1, 254)
    scaled = (w * np.exp2(127.0 - byte)[:, None, :]).reshape(k, n).astype(np.float32)
    by_word = np.ascontiguousarray(scaled.reshape(k // 512, 128, 4, n).transpose(0, 1, 3, 2))
    if fmt == "e4m3":
        words = by_word.astype(ml_dtypes.float8_e4m3fn).view(np.uint8)
    else:
        c = by_word.astype(ml_dtypes.float4_e2m1fn).view(np.uint8) & 0xF
        words = c[..., 0::2] | (c[..., 1::2] << 4)
    return np.ascontiguousarray(words), np.ascontiguousarray(byte.astype(np.uint8).reshape(k // 512, 16, n))


def unpack_weight(words, scales, fmt):
    g, p, n, _ = words.shape
    if fmt == "e4m3":
        vals = np.ascontiguousarray(words).view(ml_dtypes.float8_e4m3fn).astype(np.float64)
    else:
        nib = np.empty((g, p, n, 4), np.uint8)
        nib[..., 0::2] = words & 0xF
        nib[..., 1::2] = words >> 4
        vals = E2M1[nib]
    vals = vals * np.repeat(np.exp2(scales.astype(np.float64) - 127.0), 8, axis=1)[..., None]
    return vals.transpose(0, 1, 3, 2).reshape(g * 512, n)
def pack4(w):
    words, scales = pack_weight(w, "e2m1")
    return words.reshape(words.shape[0], 128, -1), scales


def unpack4(words, scales):
    return unpack_weight(words.reshape(words.shape[0], 128, -1, 2), scales, "e2m1")


N, D, E, SKIP = 1024, 512, 512, 512


def sigmoid(v):
    return 1.0 / (1.0 + np.exp(-v))


def draw0():
    sy, ss, t = mx_kscale(D), mx_kscale(E), mx_kscale(D)
    y = np.random.standard_normal((N, D)) * sy
    side = np.random.standard_normal((N, E)) * ss
    x = np.random.standard_normal((N, D))
    w_m = np.random.standard_normal((D, 2 * D)) / np.sqrt(D) / sy[:, None]
    w_s = np.random.standard_normal((E, 2 * D)) / np.sqrt(E) / ss[:, None]
    g = (1.0 + 0.1 * np.random.standard_normal(D)) * t
    w_o = 2.0 * np.random.standard_normal((D, D + SKIP)) / np.sqrt(D) / t[:, None]
    w_m_words, w_m_scales = pack4(w_m)
    w_s_words, w_s_scales = pack4(w_s)
    w_o_words, w_o_scales = pack4(w_o)
    return {"y": bf(y), "side": bf(side), "x": bf(x), "w_m_words": w_m_words, "w_m_scales": w_m_scales, "w_s_words": w_s_words, "w_s_scales": w_s_scales, "g": bf(g), "w_o_words": w_o_words, "w_o_scales": w_o_scales}


def core(y, side, x, w_m_words, w_m_scales, w_s_words, w_s_scales, g, w_o_words, w_o_scales):
    d = x.shape[-1]
    z = (mxq(f64(y), 1, "e4m3") @ unpack4(w_m_words, w_m_scales)) + (mxq(f64(side), 1, "e4m3") @ unpack4(w_s_words, w_s_scales))
    a = z[:, :d]
    c = z[:, d:]
    u = sigmoid(a) * np.tanh(c) * f64(g)[None, :]
    o = mxq(u, 1, "e4m3") @ unpack4(w_o_words, w_o_scales)
    xnew = (f64(x) + o[:, :d]) / np.sqrt(2.0)
    skip = o[:, d:]
    return xnew, skip


def e4m3fn_bytes(y):
    return np.clip(np.asarray(y, np.float64), -448.0, 448.0).astype(np.float32).astype(ml_dtypes.float8_e4m3fn).view(np.uint8)


def e4m3fn_values(b):
    return np.asarray(b, np.uint8).view(ml_dtypes.float8_e4m3fn).astype(np.float64)


def setup_inputs():
    d = draw0()
    x0 = np.asarray(d['y']).astype(np.float64)
    s = (np.max(np.abs(x0), axis=(0,), keepdims=True) / 448.0).astype(np.float32)
    out = {}
    for k, v in d.items():
        if k == 'y':
            out['y_bytes'] = e4m3fn_bytes(x0 / s.astype(np.float64))
            out['y_scale'] = s
        else:
            out[k] = v
    return out


def reference(y_bytes, y_scale, side, x, w_m_words, w_m_scales, w_s_words, w_s_scales, g, w_o_words, w_o_scales):
    return core(e4m3fn_values(y_bytes) * y_scale.astype(np.float64), side, x, w_m_words, w_m_scales, w_s_words, w_s_scales, g, w_o_words, w_o_scales)

@@ -1,0 +1,216 @@
+from contextlib import ExitStack
+
+import concourse.mybir as mybir
+from concourse.masks import make_identity
+
+N, D, E = 1024, 512, 512
+FLOPS = 2 * N * (D + E + D) * 2 * D
+
+F32 = mybir.dt.float32
+BF16 = mybir.dt.bfloat16
+U8 = mybir.dt.uint8
+U32 = mybir.dt.uint32
+I32 = mybir.dt.int32
+FP8 = mybir.dt.float8_e4m3fn
+FP8X4 = mybir.dt.float8_e4m3fn_x4
+FP4X4 = mybir.dt.float4_e2m1fn_x4
+MULT = mybir.AluOpType.mult
+ADD = mybir.AluOpType.add
+ACT = mybir.ActivationFunctionType
+
+P = 128
+TILES = N // P
+RSQRT2 = 0.5 ** 0.5
+
+
+def tile_csdigatedsideinforesidual_w4_kernel(tc, y_bytes, y_scale, side, x, w_m_words, w_m_scales, w_s_words, w_s_scales, g, w_o_words, w_o_scales, out_0, out_1):
+    nc = tc.nc
+    with ExitStack() as ctx:
+        keep = ctx.enter_context(tc.tile_pool(name="keep", bufs=1))
+        work = ctx.enter_context(tc.tile_pool(name="work", bufs=3))
+        psum = ctx.enter_context(tc.psum_pool(name="psum", bufs=1))
+        ctx.enter_context(tc.manual_schedule())
+
+        y_v = y_bytes.rearrange("(p i) k -> p i k", i=TILES)
+        side_v = side.rearrange("(p i) k -> p i k", i=TILES)
+        x_v = x.rearrange("(p i) k -> p i k", i=TILES)
+        xnew_v = out_0.rearrange("(p i) k -> p i k", i=TILES)
+        skip_v = out_1.rearrange("(p i) k -> p i k", i=TILES)
+
+        ys_part = keep.tile([P, 4], F32, name="ys_part")
+        g_part = keep.tile([P, 4], BF16, name="g_part")
+        ys_all = keep.tile([P, D], F32, name="ys_all", align_bytes=64)
+        y_raw = keep.tile([P, TILES, D], U8, name="y_raw", align_bytes=64)
+        side_sb = keep.tile([P, TILES, E], BF16, name="side_sb", align_bytes=64)
+        x_sb = keep.tile([P, TILES, D], BF16, name="x_sb", align_bytes=64)
+        xs_sb = keep.tile([P, TILES, D], F32, name="xs_sb", align_bytes=64)
+        ident = keep.tile([P, P], F32, name="ident")
+        warm = keep.tile([P, 1], F32, name="warm")
+        wm = keep.tile([P, 4 * D], U8, name="wm", align_bytes=64)
+        ws = keep.tile([P, 4 * D], U8, name="ws", align_bytes=64)
+        wo = keep.tile([P, 4 * D], U8, name="wo", align_bytes=64)
+        wm_sc = keep.tile([P, 2 * D], U8, name="wm_sc", align_bytes=64)
+        ws_sc = keep.tile([P, 2 * D], U8, name="ws_sc", align_bytes=64)
+        wo_sc = keep.tile([P, 2 * D], U8, name="wo_sc", align_bytes=64)
+
+        def load_scales(tile, dram):
+            for q in range(4):
+                nc.sync.dma_start(out=tile[32 * q : 32 * q + 4, :].bitcast(I32), in_=dram[0, 4 * q : 4 * q + 4, :].bitcast(I32))
+
+        def load_rows(tile, view, lo, hi):
+            nc.sync.dma_start(out=tile[:, lo:hi, :], in_=view[:, lo:hi, :])
+
+        for t in (wm_sc, ws_sc, wo_sc):
+            nc.vector.memset(t[:].bitcast(I32), 0)
+        nc.vector.memset(warm[:], 0.0)
+        nc.scalar.activation(out=warm[:], in_=warm[:], func=ACT.Sigmoid)
+        make_identity(nc, ident[:])
+
+        nc.sync.dma_start(out=ys_part[:], in_=y_scale.rearrange("o (p t) -> p (o t)", t=4))
+        load_rows(y_raw, y_v, 0, 2)
+        load_scales(wm_sc, w_m_scales)
+        load_scales(ws_sc, w_s_scales)
+        load_rows(side_sb, side_v, 0, 2)
+        nc.sync.dma_start(out=wm[:], in_=w_m_words[0])
+        nc.sync.dma_start(out=ws[:], in_=w_s_words[0])
+        nc.sync.dma_start(out=g_part[:], in_=g.rearrange("(p t) -> p t", t=4))
+        load_rows(y_raw, y_v, 2, 8)
+        load_rows(side_sb, side_v, 2, 4)
+        load_rows(side_sb, side_v, 4, 8)
+        load_rows(x_sb, x_v, 0, 4)
+        load_scales(wo_sc, w_o_scales)
+        nc.sync.dma_start(out=wo[:], in_=w_o_words[0])
+        load_rows(x_sb, x_v, 4, 8)
+
+        ys_bank = psum.tile([P, 4, P], F32, tag="ut", name="ys_bank")
+        for t in range(4):
+            nc.tensor.transpose(ys_bank[:, t, :], ys_part[:, t : t + 1].to_broadcast([P, P]), ident[:])
+        nc.scalar.copy(out=ys_all[:].rearrange("p (n t) -> p n t", t=4), in_=ys_bank[:].rearrange("p t n -> p n t"))
+
+        st = {}
+
+        def yprod(i):
+            yb = work.tile([P, D], BF16, tag="yb", name="yb", bufs=4, align_bytes=64)
+            nc.vector.tensor_tensor(out=yb[:], in0=y_raw[:, i, :].bitcast(FP8), in1=ys_all[:], op=MULT)
+            st["yb", i] = yb
+
+        def turn(i):
+            bank = psum.tile([P, 4, P], F32, tag="tb", name="tb")
+            yw = st["yb", i][:].bitcast(F32)
+            sw = side_sb[:, i, :].bitcast(F32)
+            for u in range(2):
+                nc.tensor.transpose(bank[:, 2 + u, :], sw[:, u : D // 2 : 2], ident[:])
+            for u in range(2):
+                nc.tensor.transpose(bank[:, u, :], yw[:, u : D // 2 : 2], ident[:])
+            st["tb", i] = bank
+
+        def evac(i):
+            grp = work.tile([P, 2, P, 4], BF16, tag="grp", name="grp", align_bytes=64)
+            gw = grp[:].rearrange("p o r j -> p (o r j)").bitcast(F32)
+            nc.scalar.copy(out=gw.rearrange("p (o r u) -> p o r u", o=2, u=2), in_=st["tb", i][:].rearrange("p (o u) r -> p o r u", o=2))
+            st["grp", i] = grp
+
+        def quant(i):
+            codes = work.tile([P, 2 * P], U32, tag="codes", name="codes", align_bytes=64)
+            scales = work.tile([P, 2 * P], U8, tag="scales", name="scales", align_bytes=64)
+            nc.vector.quantize_mx(out=codes[:].bitcast(FP8X4), scales=scales[:], in_=st["grp", i][:].rearrange("p o r j -> p (o r j)"))
+            st["q", i] = (codes, scales)
+
+        def mm_z(i, h):
+            codes, scales = st["q", i]
+            bank = psum.tile([P, D], F32, tag="mm", name="zb", bufs=6)
+            for o, (w, sc) in enumerate(((wm, wm_sc), (ws, ws_sc))):
+                nc.tensor.matmul_mx(
+                    out=bank[:],
+                    lhsT=codes[:, o * P : (o + 1) * P].bitcast(FP8X4),
+                    lhsT_scale=scales[:, o * P : (o + 1) * P],
+                    rhs=w[:, 2 * D * h : 2 * D * (h + 1)].bitcast(FP4X4),
+                    rhs_scale=sc[:, D * h : D * (h + 1)],
+                    start=(o == 0),
+                    stop=(o == 1),
+                )
+            st["z", h, i] = bank
+
+        def act(i, h):
+            name, func = (("sg", ACT.Sigmoid), ("th", ACT.Tanh))[h]
+            r = work.tile([P, 4, P], F32, tag=name, name=name, align_bytes=64)
+            nc.scalar.activation(out=r[:], in_=st["z", h, i][:].rearrange("p (m t) -> p t m", t=4), func=func)
+            st[name, i] = r
+
+        def uprod(i):
+            u = work.tile([P, 4, P], F32, tag="u", name="u", align_bytes=64)
+            nc.vector.tensor_tensor(out=u[:], in0=st["sg", i][:], in1=st["th", i][:], op=MULT)
+            st["u", i] = u
+
+        def turn_u(i):
+            bank = psum.tile([P, 4, P], F32, tag="ut", name="ut")
+            for t in range(4):
+                nc.tensor.transpose(bank[:, t, :], st["u", i][:, t, :], ident[:])
+            st["ut", i] = bank
+
+        def gain(i):
+            ug = work.tile([P, P, 4], BF16, tag="ug", name="ug", align_bytes=64)
+            nc.vector.tensor_tensor(
+                out=ug[:],
+                in0=st["ut", i][:].rearrange("p t r -> p r t"),
+                in1=g_part[:].unsqueeze(1).to_broadcast([P, P, 4]),
+                op=MULT,
+            )
+            st["ug", i] = ug
+
+        def quant_u(i):
+            codes = work.tile([P, P], U32, tag="ucodes", name="ucodes", bufs=4, align_bytes=64)
+            scales = work.tile([P, P], U8, tag="uscales", name="uscales", bufs=4, align_bytes=64)
+            nc.vector.quantize_mx(out=codes[:].bitcast(FP8X4), scales=scales[:], in_=st["ug", i][:].rearrange("p r t -> p (r t)"))
+            st["uq", i] = (codes, scales)
+
+        def mm_o(i, h):
+            codes, scales = st["uq", i]
+            bank = psum.tile([P, D], F32, tag="mm", name="ob", bufs=6)
+            nc.tensor.matmul_mx(
+                out=bank[:],
+                lhsT=codes[:].bitcast(FP8X4),
+                lhsT_scale=scales[:],
+                rhs=wo[:, 2 * D * h : 2 * D * (h + 1)].bitcast(FP4X4),
+                rhs_scale=wo_sc[:, D * h : D * (h + 1)],
+                start=True,
+                stop=True,
+            )
+            st["o", h, i] = bank
+
+        def scale_x(i):
+            nc.scalar.activation(out=xs_sb[:, i, :], in_=x_sb[:, i, :], func=ACT.Copy, scale=RSQRT2)
+
+        def skip(i):
+            r = work.tile([P, D], F32, tag="sk", name="sk", align_bytes=64)
+            nc.scalar.copy(out=r[:], in_=st["o", 1, i][:])
+            nc.sync.dma_start(out=skip_v[:, i, :], in_=r[:])
+
+        def xnew(i):
+            r = work.tile([P, D], F32, tag="xn", name="xn", align_bytes=64)
+            nc.vector.scalar_tensor_tensor(out=r[:], in0=st["o", 0, i][:], scalar=RSQRT2, in1=xs_sb[:, i, :], op0=MULT, op1=ADD)
+            nc.sync.dma_start(out=xnew_v[:, i, :], in_=r[:])
+
+        order = (
+            (turn_u, 2),
+            (turn, -1),
+            (scale_x, 2),
+            (evac, -1),
+            (yprod, -2),
+            (mm_z, 0, 0),
+            (mm_z, 0, 1),
+            (mm_o, 4, 0),
+            (act, 0, 0),
+            (gain, 2),
+            (act, 0, 1),
+            (uprod, 1),
+            (quant_u, 2),
+            (quant, -1),
+            (skip, 5),
+            (mm_o, 4, 1),
+            (xnew, 4),
+        )
+        for s in range(-2, TILES + 5):
+            for stage, lag, *args in order:
+                if 0 <= s - lag < TILES:
+                    stage(s - lag, *args)

@@ -21,6 +21,8 @@ ACT = mybir.ActivationFunctionType
 P = 128
 TILES = N // P
 RSQRT2 = 0.5 ** 0.5
+EARLY = 2
+TB = 2
 
 
 def tile_csdigatedsideinforesidual_w4_kernel(tc, y_bytes, y_scale, side, x, w_m_words, w_m_scales, w_s_words, w_s_scales, g, w_o_words, w_o_scales, out_0, out_1):
@@ -60,21 +62,20 @@ def tile_csdigatedsideinforesidual_w4_kernel(tc, y_bytes, y_scale, side, x, w_m_
         def load_rows(tile, view, lo, hi):
             nc.sync.dma_start(out=tile[:, lo:hi, :], in_=view[:, lo:hi, :])
 
-        for t in (wm_sc, ws_sc, wo_sc):
-            nc.vector.memset(t[:].bitcast(I32), 0)
-        nc.vector.memset(warm[:], 0.0)
-        nc.scalar.activation(out=warm[:], in_=warm[:], func=ACT.Sigmoid)
+        nc.gpsimd.dma_start(out=ys_part[:], in_=y_scale.rearrange("o (p t) -> p (o t)", t=4))
         make_identity(nc, ident[:])
+        nc.gpsimd.dma_start(out=g_part[:], in_=g.rearrange("(p t) -> p t", t=4))
+        for t in (warm, wm_sc, ws_sc, wo_sc):
+            nc.vector.memset(t[:].bitcast(I32), 0)
+        nc.scalar.activation(out=warm[:], in_=warm[:], func=ACT.Sigmoid)
 
-        nc.sync.dma_start(out=ys_part[:], in_=y_scale.rearrange("o (p t) -> p (o t)", t=4))
         load_rows(y_raw, y_v, 0, 2)
-        load_scales(wm_sc, w_m_scales)
-        load_scales(ws_sc, w_s_scales)
         load_rows(side_sb, side_v, 0, 2)
         nc.sync.dma_start(out=wm[:], in_=w_m_words[0])
-        nc.sync.dma_start(out=ws[:], in_=w_s_words[0])
-        nc.sync.dma_start(out=g_part[:], in_=g.rearrange("(p t) -> p t", t=4))
+        load_scales(wm_sc, w_m_scales)
         load_rows(y_raw, y_v, 2, 8)
+        nc.sync.dma_start(out=ws[:], in_=w_s_words[0])
+        load_scales(ws_sc, w_s_scales)
         load_rows(side_sb, side_v, 2, 4)
         load_rows(side_sb, side_v, 4, 8)
         load_rows(x_sb, x_v, 0, 4)
@@ -82,33 +83,53 @@ def tile_csdigatedsideinforesidual_w4_kernel(tc, y_bytes, y_scale, side, x, w_m_
         nc.sync.dma_start(out=wo[:], in_=w_o_words[0])
         load_rows(x_sb, x_v, 4, 8)
 
-        ys_bank = psum.tile([P, 4, P], F32, tag="ut", name="ys_bank")
-        for t in range(4):
-            nc.tensor.transpose(ys_bank[:, t, :], ys_part[:, t : t + 1].to_broadcast([P, P]), ident[:])
-        nc.scalar.copy(out=ys_all[:].rearrange("p (n t) -> p n t", t=4), in_=ys_bank[:].rearrange("p t n -> p n t"))
-
         st = {}
+
+        def spread_scales():
+            bank = psum.tile([P, 4, P], F32, tag="mm", name="ysb", bufs=8 - TB)
+            for t in range(4):
+                nc.tensor.transpose(bank[:, t, :], ys_part[:, t : t + 1].to_broadcast([P, P]), ident[:])
+            nc.scalar.copy(out=ys_all[:].rearrange("p (n t) -> p n t", t=4), in_=bank[:].rearrange("p t n -> p n t"))
 
         def yprod(i):
             yb = work.tile([P, D], BF16, tag="yb", name="yb", bufs=4, align_bytes=64)
-            nc.vector.tensor_tensor(out=yb[:], in0=y_raw[:, i, :].bitcast(FP8), in1=ys_all[:], op=MULT)
+            if i < EARLY:
+                nc.vector.tensor_copy(out=yb[:], in_=y_raw[:, i, :].bitcast(FP8))
+            else:
+                nc.vector.tensor_tensor(out=yb[:], in0=y_raw[:, i, :].bitcast(FP8), in1=ys_all[:], op=MULT)
             st["yb", i] = yb
 
         def turn(i):
-            bank = psum.tile([P, 4, P], F32, tag="tb", name="tb")
             yw = st["yb", i][:].bitcast(F32)
             sw = side_sb[:, i, :].bitcast(F32)
-            for u in range(2):
-                nc.tensor.transpose(bank[:, 2 + u, :], sw[:, u : D // 2 : 2], ident[:])
+            bank = psum.tile([P, 4, P], F32, tag="t", name="tb", bufs=TB)
+            sbank = psum.tile([P, 4, P], F32, tag="mm", name="tsb", bufs=8 - TB) if i < EARLY else bank
             for u in range(2):
                 nc.tensor.transpose(bank[:, u, :], yw[:, u : D // 2 : 2], ident[:])
-            st["tb", i] = bank
+            for u in range(2):
+                nc.tensor.transpose(sbank[:, 2 + u, :], sw[:, u : D // 2 : 2], ident[:])
+            st["tb", i] = (bank, sbank)
+            st["grp", i] = work.tile([P, 2, P, 4], BF16, tag="grp", name="grp", align_bytes=64)
 
         def evac(i):
-            grp = work.tile([P, 2, P, 4], BF16, tag="grp", name="grp", align_bytes=64)
-            gw = grp[:].rearrange("p o r j -> p (o r j)").bitcast(F32)
-            nc.scalar.copy(out=gw.rearrange("p (o r u) -> p o r u", o=2, u=2), in_=st["tb", i][:].rearrange("p (o u) r -> p o r u", o=2))
-            st["grp", i] = grp
+            bank, sbank = st["tb", i]
+            lo = 1 if i < EARLY else 0
+            gw = st["grp", i][:].rearrange("p o r j -> p (o r j)").bitcast(F32)
+            nc.scalar.copy(
+                out=gw.rearrange("p (o r u) -> p o r u", o=2, u=2)[:, lo:],
+                in_=sbank[:].rearrange("p (o u) r -> p o r u", o=2)[:, lo:],
+            )
+
+        def evac_y(i):
+            if i < EARLY:
+                bank, sbank = st["tb", i]
+                yt = bank[:, 0:2, :].rearrange("p u r -> p (u r)").bitcast(BF16)
+                nc.vector.tensor_tensor(
+                    out=st["grp", i][:, 0].rearrange("p r (u e) -> p r u e", e=2),
+                    in0=yt.rearrange("p (u r e) -> p r u e", u=2, e=2),
+                    in1=ys_part[:].rearrange("p (u e) -> p u e", e=2).unsqueeze(1).to_broadcast([P, P, 2, 2]),
+                    op=MULT,
+                )
 
         def quant(i):
             codes = work.tile([P, 2 * P], U32, tag="codes", name="codes", align_bytes=64)
@@ -118,7 +139,7 @@ def tile_csdigatedsideinforesidual_w4_kernel(tc, y_bytes, y_scale, side, x, w_m_
 
         def mm_z(i, h):
             codes, scales = st["q", i]
-            bank = psum.tile([P, D], F32, tag="mm", name="zb", bufs=6)
+            bank = psum.tile([P, D], F32, tag="mm", name="zb", bufs=8 - TB)
             for o, (w, sc) in enumerate(((wm, wm_sc), (ws, ws_sc))):
                 nc.tensor.matmul_mx(
                     out=bank[:],
@@ -143,7 +164,7 @@ def tile_csdigatedsideinforesidual_w4_kernel(tc, y_bytes, y_scale, side, x, w_m_
             st["u", i] = u
 
         def turn_u(i):
-            bank = psum.tile([P, 4, P], F32, tag="ut", name="ut")
+            bank = psum.tile([P, 4, P], F32, tag="t", name="ut", bufs=TB)
             for t in range(4):
                 nc.tensor.transpose(bank[:, t, :], st["u", i][:, t, :], ident[:])
             st["ut", i] = bank
@@ -159,14 +180,14 @@ def tile_csdigatedsideinforesidual_w4_kernel(tc, y_bytes, y_scale, side, x, w_m_
             st["ug", i] = ug
 
         def quant_u(i):
-            codes = work.tile([P, P], U32, tag="ucodes", name="ucodes", bufs=4, align_bytes=64)
-            scales = work.tile([P, P], U8, tag="uscales", name="uscales", bufs=4, align_bytes=64)
+            codes = work.tile([P, P], U32, tag="ucodes", name="ucodes", bufs=6, align_bytes=64)
+            scales = work.tile([P, P], U8, tag="uscales", name="uscales", bufs=6, align_bytes=64)
             nc.vector.quantize_mx(out=codes[:].bitcast(FP8X4), scales=scales[:], in_=st["ug", i][:].rearrange("p r t -> p (r t)"))
             st["uq", i] = (codes, scales)
 
         def mm_o(i, h):
             codes, scales = st["uq", i]
-            bank = psum.tile([P, D], F32, tag="mm", name="ob", bufs=6)
+            bank = psum.tile([P, D], F32, tag="mm", name="ob", bufs=8 - TB)
             nc.tensor.matmul_mx(
                 out=bank[:],
                 lhsT=codes[:].bitcast(FP8X4),
@@ -191,26 +212,34 @@ def tile_csdigatedsideinforesidual_w4_kernel(tc, y_bytes, y_scale, side, x, w_m_
             nc.vector.scalar_tensor_tensor(out=r[:], in0=st["o", 0, i][:], scalar=RSQRT2, in1=xs_sb[:, i, :], op0=MULT, op1=ADD)
             nc.sync.dma_start(out=xnew_v[:, i, :], in_=r[:])
 
+        yprod(0)
+        yprod(1)
+        turn(0)
+        spread_scales()
+        evac_y(0)
+        evac(0)
+        done = {(yprod, 0), (yprod, 1), (turn, 0), (evac_y, 0), (evac, 0)}
         order = (
-            (turn_u, 2),
+            (quant_u, 3),
+            (skip, 5),
             (turn, -1),
+            (turn_u, 2),
             (scale_x, 2),
-            (evac, -1),
+            (xnew, 4),
             (yprod, -2),
-            (mm_z, 0, 0),
             (mm_z, 0, 1),
-            (mm_o, 4, 0),
-            (act, 0, 0),
-            (gain, 2),
+            (evac, -1),
+            (evac_y, -1),
+            (mm_z, 0, 0),
+            (mm_o, 4, 1),
+            (mm_o, 3, 0),
             (act, 0, 1),
             (uprod, 1),
-            (quant_u, 2),
+            (gain, 2),
+            (act, 0, 0),
             (quant, -1),
-            (skip, 5),
-            (mm_o, 4, 1),
-            (xnew, 4),
         )
         for s in range(-2, TILES + 5):
             for stage, lag, *args in order:
-                if 0 <= s - lag < TILES:
+                if 0 <= s - lag < TILES and (stage, s - lag) not in done:
                     stage(s - lag, *args)

@@ -47,6 +47,7 @@ def tile_csdigatedsideinforesidual_w4_kernel(tc, y_bytes, y_scale, side, x, w_m_
         x_sb = keep.tile([P, TILES, D], BF16, name="x_sb", align_bytes=64)
         xs_sb = keep.tile([P, TILES, D], F32, name="xs_sb", align_bytes=64)
         ident = keep.tile([P, P], F32, name="ident")
+        zeros = keep.tile([P, D], BF16, name="zeros", align_bytes=64)
         warm = keep.tile([P, 1], F32, name="warm")
         wm = keep.tile([P, 4 * D], U8, name="wm", align_bytes=64)
         ws = keep.tile([P, 4 * D], U8, name="ws", align_bytes=64)
@@ -62,26 +63,33 @@ def tile_csdigatedsideinforesidual_w4_kernel(tc, y_bytes, y_scale, side, x, w_m_
         def load_rows(tile, view, lo, hi):
             nc.sync.dma_start(out=tile[:, lo:hi, :], in_=view[:, lo:hi, :])
 
-        nc.gpsimd.dma_start(out=ys_part[:], in_=y_scale.rearrange("o (p t) -> p (o t)", t=4))
+        nc.gpsimd.memset(zeros[:].bitcast(I32), 0)
         make_identity(nc, ident[:])
-        nc.gpsimd.dma_start(out=g_part[:], in_=g.rearrange("(p t) -> p t", t=4))
-        for t in (warm, wm_sc, ws_sc, wo_sc):
+        for t in (wm_sc, ws_sc, warm, wo_sc):
             nc.vector.memset(t[:].bitcast(I32), 0)
         nc.scalar.activation(out=warm[:], in_=warm[:], func=ACT.Sigmoid)
 
-        load_rows(y_raw, y_v, 0, 2)
+        load_rows(y_raw, y_v, 0, 3)
         load_rows(side_sb, side_v, 0, 2)
-        nc.sync.dma_start(out=wm[:], in_=w_m_words[0])
+        nc.sync.dma_start(out=ys_part[:], in_=y_scale.rearrange("o (p t) -> p (o t)", t=4))
         load_scales(wm_sc, w_m_scales)
-        load_rows(y_raw, y_v, 2, 8)
-        nc.sync.dma_start(out=ws[:], in_=w_s_words[0])
         load_scales(ws_sc, w_s_scales)
+        nc.sync.dma_start(out=wm[:], in_=w_m_words[0])
+        nc.sync.dma_start(out=ws[:], in_=w_s_words[0])
+        load_rows(y_raw, y_v, 3, 8)
         load_rows(side_sb, side_v, 2, 4)
+        nc.sync.dma_start(out=g_part[:], in_=g.rearrange("(p t) -> p t", t=4))
         load_rows(side_sb, side_v, 4, 8)
         load_rows(x_sb, x_v, 0, 4)
         load_scales(wo_sc, w_o_scales)
         nc.sync.dma_start(out=wo[:], in_=w_o_words[0])
         load_rows(x_sb, x_v, 4, 8)
+
+        warm_bank = psum.tile([P, D], F32, tag="mm", name="warm_bank", bufs=8 - TB)
+
+        def warm_up(n):
+            for k in range(n):
+                nc.tensor.matmul(warm_bank[:], lhsT=zeros[:, 0:P], rhs=zeros[:], start=True, stop=True)
 
         st = {}
 
@@ -212,34 +220,39 @@ def tile_csdigatedsideinforesidual_w4_kernel(tc, y_bytes, y_scale, side, x, w_m_
             nc.vector.scalar_tensor_tensor(out=r[:], in0=st["o", 0, i][:], scalar=RSQRT2, in1=xs_sb[:, i, :], op0=MULT, op1=ADD)
             nc.sync.dma_start(out=xnew_v[:, i, :], in_=r[:])
 
+        warm_up(4)
         yprod(0)
         yprod(1)
         turn(0)
+        warm_up(1)
         spread_scales()
+        warm_up(1)
         evac_y(0)
         evac(0)
-        done = {(yprod, 0), (yprod, 1), (turn, 0), (evac_y, 0), (evac, 0)}
+        turn(1)
+        warm_up(1)
+        done = {(yprod, 0), (yprod, 1), (turn, 0), (turn, 1), (evac_y, 0), (evac, 0)}
         order = (
-            (quant_u, 3),
-            (skip, 5),
+            (mm_o, 4, 0),
             (turn, -1),
-            (turn_u, 2),
-            (scale_x, 2),
-            (xnew, 4),
-            (yprod, -2),
-            (mm_z, 0, 1),
             (evac, -1),
-            (evac_y, -1),
+            (turn_u, 2),
+            (quant_u, 3),
+            (xnew, 4),
+            (scale_x, 2),
+            (mm_z, 0, 1),
+            (yprod, -2),
             (mm_z, 0, 0),
-            (mm_o, 4, 1),
-            (mm_o, 3, 0),
             (act, 0, 1),
-            (uprod, 1),
-            (gain, 2),
+            (mm_o, 4, 1),
             (act, 0, 0),
+            (skip, 4),
+            (uprod, 1),
+            (evac_y, -1),
+            (gain, 2),
             (quant, -1),
         )
-        for s in range(-2, TILES + 5):
+        for s in range(-2, TILES + 4):
             for stage, lag, *args in order:
                 if 0 <= s - lag < TILES and (stage, s - lag) not in done:
                     stage(s - lag, *args)

@@ -22,14 +22,13 @@ P = 128
 TILES = N // P
 RSQRT2 = 0.5 ** 0.5
 EARLY = 2
-TB = 2
 
 
 def tile_csdigatedsideinforesidual_w4_kernel(tc, y_bytes, y_scale, side, x, w_m_words, w_m_scales, w_s_words, w_s_scales, g, w_o_words, w_o_scales, out_0, out_1):
     nc = tc.nc
     with ExitStack() as ctx:
         keep = ctx.enter_context(tc.tile_pool(name="keep", bufs=1))
-        work = ctx.enter_context(tc.tile_pool(name="work", bufs=3))
+        work = ctx.enter_context(tc.tile_pool(name="work", bufs=4))
         psum = ctx.enter_context(tc.psum_pool(name="psum", bufs=1))
         ctx.enter_context(tc.manual_schedule())
 
@@ -65,27 +64,27 @@ def tile_csdigatedsideinforesidual_w4_kernel(tc, y_bytes, y_scale, side, x, w_m_
 
         nc.gpsimd.memset(zeros[:].bitcast(I32), 0)
         make_identity(nc, ident[:])
+        nc.gpsimd.dma_start(out=side_sb[:, 2:4, :], in_=side_v[:, 2:4, :])
         for t in (wm_sc, ws_sc, warm, wo_sc):
             nc.vector.memset(t[:].bitcast(I32), 0)
         nc.scalar.activation(out=warm[:], in_=warm[:], func=ACT.Sigmoid)
 
-        load_rows(y_raw, y_v, 0, 3)
-        load_rows(side_sb, side_v, 0, 2)
         nc.sync.dma_start(out=ys_part[:], in_=y_scale.rearrange("o (p t) -> p (o t)", t=4))
+        load_rows(y_raw, y_v, 0, 4)
+        load_rows(side_sb, side_v, 0, 2)
         load_scales(wm_sc, w_m_scales)
         load_scales(ws_sc, w_s_scales)
         nc.sync.dma_start(out=wm[:], in_=w_m_words[0])
         nc.sync.dma_start(out=ws[:], in_=w_s_words[0])
-        load_rows(y_raw, y_v, 3, 8)
-        load_rows(side_sb, side_v, 2, 4)
-        nc.sync.dma_start(out=g_part[:], in_=g.rearrange("(p t) -> p t", t=4))
+        load_rows(y_raw, y_v, 4, 8)
         load_rows(side_sb, side_v, 4, 8)
+        nc.sync.dma_start(out=g_part[:], in_=g.rearrange("(p t) -> p t", t=4))
         load_rows(x_sb, x_v, 0, 4)
         load_scales(wo_sc, w_o_scales)
         nc.sync.dma_start(out=wo[:], in_=w_o_words[0])
         load_rows(x_sb, x_v, 4, 8)
 
-        warm_bank = psum.tile([P, D], F32, tag="mm", name="warm_bank", bufs=8 - TB)
+        warm_bank = psum.tile([P, D], F32, tag="bank", name="warm_bank", bufs=8)
 
         def warm_up(n):
             for k in range(n):
@@ -94,13 +93,13 @@ def tile_csdigatedsideinforesidual_w4_kernel(tc, y_bytes, y_scale, side, x, w_m_
         st = {}
 
         def spread_scales():
-            bank = psum.tile([P, 4, P], F32, tag="mm", name="ysb", bufs=8 - TB)
+            bank = psum.tile([P, 4, P], F32, tag="bank", name="ysb", bufs=8)
             for t in range(4):
                 nc.tensor.transpose(bank[:, t, :], ys_part[:, t : t + 1].to_broadcast([P, P]), ident[:])
             nc.scalar.copy(out=ys_all[:].rearrange("p (n t) -> p n t", t=4), in_=bank[:].rearrange("p t n -> p n t"))
 
         def yprod(i):
-            yb = work.tile([P, D], BF16, tag="yb", name="yb", bufs=4, align_bytes=64)
+            yb = work.tile([P, D], BF16, tag="yb", name="yb", bufs=6, align_bytes=64)
             if i < EARLY:
                 nc.vector.tensor_copy(out=yb[:], in_=y_raw[:, i, :].bitcast(FP8))
             else:
@@ -110,14 +109,14 @@ def tile_csdigatedsideinforesidual_w4_kernel(tc, y_bytes, y_scale, side, x, w_m_
         def turn(i):
             yw = st["yb", i][:].bitcast(F32)
             sw = side_sb[:, i, :].bitcast(F32)
-            bank = psum.tile([P, 4, P], F32, tag="t", name="tb", bufs=TB)
-            sbank = psum.tile([P, 4, P], F32, tag="mm", name="tsb", bufs=8 - TB) if i < EARLY else bank
+            bank = psum.tile([P, 4, P], F32, tag="bank", name="tb", bufs=8)
+            sbank = psum.tile([P, 4, P], F32, tag="bank", name="tsb", bufs=8) if i < EARLY else bank
             for u in range(2):
                 nc.tensor.transpose(bank[:, u, :], yw[:, u : D // 2 : 2], ident[:])
             for u in range(2):
                 nc.tensor.transpose(sbank[:, 2 + u, :], sw[:, u : D // 2 : 2], ident[:])
             st["tb", i] = (bank, sbank)
-            st["grp", i] = work.tile([P, 2, P, 4], BF16, tag="grp", name="grp", align_bytes=64)
+            st["grp", i] = work.tile([P, 2, P, 4], BF16, tag="grp", name="grp", bufs=6, align_bytes=64)
 
         def evac(i):
             bank, sbank = st["tb", i]
@@ -147,7 +146,7 @@ def tile_csdigatedsideinforesidual_w4_kernel(tc, y_bytes, y_scale, side, x, w_m_
 
         def mm_z(i, h):
             codes, scales = st["q", i]
-            bank = psum.tile([P, D], F32, tag="mm", name="zb", bufs=8 - TB)
+            bank = psum.tile([P, D], F32, tag="bank", name="zb", bufs=8)
             for o, (w, sc) in enumerate(((wm, wm_sc), (ws, ws_sc))):
                 nc.tensor.matmul_mx(
                     out=bank[:],
@@ -172,7 +171,7 @@ def tile_csdigatedsideinforesidual_w4_kernel(tc, y_bytes, y_scale, side, x, w_m_
             st["u", i] = u
 
         def turn_u(i):
-            bank = psum.tile([P, 4, P], F32, tag="t", name="ut", bufs=TB)
+            bank = psum.tile([P, 4, P], F32, tag="bank", name="ut", bufs=8)
             for t in range(4):
                 nc.tensor.transpose(bank[:, t, :], st["u", i][:, t, :], ident[:])
             st["ut", i] = bank
@@ -195,7 +194,7 @@ def tile_csdigatedsideinforesidual_w4_kernel(tc, y_bytes, y_scale, side, x, w_m_
 
         def mm_o(i, h):
             codes, scales = st["uq", i]
-            bank = psum.tile([P, D], F32, tag="mm", name="ob", bufs=8 - TB)
+            bank = psum.tile([P, D], F32, tag="bank", name="ob", bufs=8)
             nc.tensor.matmul_mx(
                 out=bank[:],
                 lhsT=codes[:].bitcast(FP8X4),
@@ -220,39 +219,61 @@ def tile_csdigatedsideinforesidual_w4_kernel(tc, y_bytes, y_scale, side, x, w_m_
             nc.vector.scalar_tensor_tensor(out=r[:], in0=st["o", 0, i][:], scalar=RSQRT2, in1=xs_sb[:, i, :], op0=MULT, op1=ADD)
             nc.sync.dma_start(out=xnew_v[:, i, :], in_=r[:])
 
-        warm_up(4)
+        warm_up(3)
+        spread_scales()
+        warm_up(1)
         yprod(0)
         yprod(1)
         turn(0)
-        warm_up(1)
-        spread_scales()
-        warm_up(1)
-        evac_y(0)
-        evac(0)
+        yprod(2)
         turn(1)
-        warm_up(1)
-        done = {(yprod, 0), (yprod, 1), (turn, 0), (turn, 1), (evac_y, 0), (evac, 0)}
+        evac(0)
+        evac_y(0)
+        turn(2)
+        warm_up(2)
+        yprod(3)
+        quant(0)
+        evac(1)
+        evac_y(1)
+        done = {(yprod, 0), (yprod, 1), (yprod, 2), (yprod, 3), (turn, 0), (turn, 1), (turn, 2), (evac, 0), (evac, 1), (quant, 0)}
         order = (
-            (mm_o, 4, 0),
-            (turn, -1),
-            (evac, -1),
-            (turn_u, 2),
-            (quant_u, 3),
-            (xnew, 4),
-            (scale_x, 2),
-            (mm_z, 0, 1),
-            (yprod, -2),
-            (mm_z, 0, 0),
-            (act, 0, 1),
-            (mm_o, 4, 1),
-            (act, 0, 0),
+            (mm_z, -1, 1),
+            (mm_z, -1, 0),
+            (quant, -2),
+            (turn, -4),
             (skip, 4),
-            (uprod, 1),
-            (evac_y, -1),
-            (gain, 2),
-            (quant, -1),
+            (turn_u, 1),
+            (turn, -5),
+            (xnew, 4),
+            (uprod, 0),
+            (quant_u, 2),
+            (quant, -3),
+            (act, -1, 1),
+            (turn_u, 0),
+            (mm_z, -2, 0),
+            (act, -1, 0),
+            (evac, -4),
+            (scale_x, 0),
+            (evac, -5),
+            (yprod, -7),
+            (xnew, 3),
+            (gain, 1),
+            (gain, 0),
+            (mm_z, -2, 1),
+            (quant_u, 1),
+            (act, -2, 0),
+            (mm_o, 3, 1),
+            (act, -2, 1),
+            (mm_o, 2, 0),
+            (skip, 3),
+            (uprod, -1),
+            (mm_o, 2, 1),
+            (scale_x, 1),
+            (yprod, -6),
+            (mm_o, 1, 0),
         )
-        for s in range(-2, TILES + 4):
+        for s in range(-5, 8):
             for stage, lag, *args in order:
-                if 0 <= s - lag < TILES and (stage, s - lag) not in done:
-                    stage(s - lag, *args)
+                i = 2 * s - lag
+                if 0 <= i < TILES and (stage, i) not in done:
+                    stage(i, *args)

from contextlib import ExitStack

import concourse.mybir as mybir
from concourse.masks import make_identity

N, D, E = 1024, 512, 512
FLOPS = 2 * N * (D + E + D) * 2 * D

F32 = mybir.dt.float32
BF16 = mybir.dt.bfloat16
U8 = mybir.dt.uint8
U32 = mybir.dt.uint32
I32 = mybir.dt.int32
FP8 = mybir.dt.float8_e4m3fn
FP8X4 = mybir.dt.float8_e4m3fn_x4
FP4X4 = mybir.dt.float4_e2m1fn_x4
MULT = mybir.AluOpType.mult
ADD = mybir.AluOpType.add
ACT = mybir.ActivationFunctionType

P = 128
TILES = N // P
RSQRT2 = 0.5 ** 0.5
EARLY = 2


def tile_csdigatedsideinforesidual_w4_kernel(tc, y_bytes, y_scale, side, x, w_m_words, w_m_scales, w_s_words, w_s_scales, g, w_o_words, w_o_scales, out_0, out_1):
    nc = tc.nc
    with ExitStack() as ctx:
        keep = ctx.enter_context(tc.tile_pool(name="keep", bufs=1))
        work = ctx.enter_context(tc.tile_pool(name="work", bufs=4))
        psum = ctx.enter_context(tc.psum_pool(name="psum", bufs=1))
        ctx.enter_context(tc.manual_schedule())

        y_v = y_bytes.rearrange("(p i) k -> p i k", i=TILES)
        side_v = side.rearrange("(p i) k -> p i k", i=TILES)
        x_v = x.rearrange("(p i) k -> p i k", i=TILES)
        xnew_v = out_0.rearrange("(p i) k -> p i k", i=TILES)
        skip_v = out_1.rearrange("(p i) k -> p i k", i=TILES)

        ys_part = keep.tile([P, 4], F32, name="ys_part")
        g_part = keep.tile([P, 4], BF16, name="g_part")
        ys_all = keep.tile([P, D], F32, name="ys_all", align_bytes=64)
        y_raw = keep.tile([P, TILES, D], U8, name="y_raw", align_bytes=64)
        side_sb = keep.tile([P, TILES, E], BF16, name="side_sb", align_bytes=64)
        x_sb = keep.tile([P, TILES, D], BF16, name="x_sb", align_bytes=64)
        xs_sb = keep.tile([P, TILES, D], F32, name="xs_sb", align_bytes=64)
        ident = keep.tile([P, P], F32, name="ident")
        zeros = keep.tile([P, D], BF16, name="zeros", align_bytes=64)
        warm = keep.tile([P, 1], F32, name="warm")
        wm = keep.tile([P, 4 * D], U8, name="wm", align_bytes=64)
        ws = keep.tile([P, 4 * D], U8, name="ws", align_bytes=64)
        wo = keep.tile([P, 4 * D], U8, name="wo", align_bytes=64)
        wm_sc = keep.tile([P, 2 * D], U8, name="wm_sc", align_bytes=64)
        ws_sc = keep.tile([P, 2 * D], U8, name="ws_sc", align_bytes=64)
        wo_sc = keep.tile([P, 2 * D], U8, name="wo_sc", align_bytes=64)

        def load_scales(tile, dram):
            for q in range(4):
                nc.sync.dma_start(out=tile[32 * q : 32 * q + 4, :].bitcast(I32), in_=dram[0, 4 * q : 4 * q + 4, :].bitcast(I32))

        def load_rows(tile, view, lo, hi):
            nc.sync.dma_start(out=tile[:, lo:hi, :], in_=view[:, lo:hi, :])

        nc.gpsimd.memset(zeros[:].bitcast(I32), 0)
        make_identity(nc, ident[:])
        nc.gpsimd.dma_start(out=side_sb[:, 2:4, :], in_=side_v[:, 2:4, :])
        for t in (wm_sc, ws_sc, warm, wo_sc):
            nc.vector.memset(t[:].bitcast(I32), 0)
        nc.scalar.activation(out=warm[:], in_=warm[:], func=ACT.Sigmoid)

        nc.sync.dma_start(out=ys_part[:], in_=y_scale.rearrange("o (p t) -> p (o t)", t=4))
        load_rows(y_raw, y_v, 0, 4)
        load_rows(side_sb, side_v, 0, 2)
        load_scales(wm_sc, w_m_scales)
        load_scales(ws_sc, w_s_scales)
        nc.sync.dma_start(out=wm[:], in_=w_m_words[0])
        nc.sync.dma_start(out=ws[:], in_=w_s_words[0])
        load_rows(y_raw, y_v, 4, 8)
        load_rows(side_sb, side_v, 4, 8)
        nc.sync.dma_start(out=g_part[:], in_=g.rearrange("(p t) -> p t", t=4))
        load_rows(x_sb, x_v, 0, 4)
        load_scales(wo_sc, w_o_scales)
        nc.sync.dma_start(out=wo[:], in_=w_o_words[0])
        load_rows(x_sb, x_v, 4, 8)

        warm_bank = psum.tile([P, D], F32, tag="bank", name="warm_bank", bufs=8)

        def warm_up(n):
            for k in range(n):
                nc.tensor.matmul(warm_bank[:], lhsT=zeros[:, 0:P], rhs=zeros[:], start=True, stop=True)

        st = {}

        def spread_scales():
            bank = psum.tile([P, 4, P], F32, tag="bank", name="ysb", bufs=8)
            for t in range(4):
                nc.tensor.transpose(bank[:, t, :], ys_part[:, t : t + 1].to_broadcast([P, P]), ident[:])
            nc.scalar.copy(out=ys_all[:].rearrange("p (n t) -> p n t", t=4), in_=bank[:].rearrange("p t n -> p n t"))

        def yprod(i):
            yb = work.tile([P, D], BF16, tag="yb", name="yb", bufs=6, align_bytes=64)
            if i < EARLY:
                nc.vector.tensor_copy(out=yb[:], in_=y_raw[:, i, :].bitcast(FP8))
            else:
                nc.vector.tensor_tensor(out=yb[:], in0=y_raw[:, i, :].bitcast(FP8), in1=ys_all[:], op=MULT)
            st["yb", i] = yb

        def turn(i):
            yw = st["yb", i][:].bitcast(F32)
            sw = side_sb[:, i, :].bitcast(F32)
            bank = psum.tile([P, 4, P], F32, tag="bank", name="tb", bufs=8)
            sbank = psum.tile([P, 4, P], F32, tag="bank", name="tsb", bufs=8) if i < EARLY else bank
            for u in range(2):
                nc.tensor.transpose(bank[:, u, :], yw[:, u : D // 2 : 2], ident[:])
            for u in range(2):
                nc.tensor.transpose(sbank[:, 2 + u, :], sw[:, u : D // 2 : 2], ident[:])
            st["tb", i] = (bank, sbank)
            st["grp", i] = work.tile([P, 2, P, 4], BF16, tag="grp", name="grp", bufs=6, align_bytes=64)

        def evac(i):
            bank, sbank = st["tb", i]
            lo = 1 if i < EARLY else 0
            gw = st["grp", i][:].rearrange("p o r j -> p (o r j)").bitcast(F32)
            nc.scalar.copy(
                out=gw.rearrange("p (o r u) -> p o r u", o=2, u=2)[:, lo:],
                in_=sbank[:].rearrange("p (o u) r -> p o r u", o=2)[:, lo:],
            )

        def evac_y(i):
            if i < EARLY:
                bank, sbank = st["tb", i]
                yt = bank[:, 0:2, :].rearrange("p u r -> p (u r)").bitcast(BF16)
                nc.vector.tensor_tensor(
                    out=st["grp", i][:, 0].rearrange("p r (u e) -> p r u e", e=2),
                    in0=yt.rearrange("p (u r e) -> p r u e", u=2, e=2),
                    in1=ys_part[:].rearrange("p (u e) -> p u e", e=2).unsqueeze(1).to_broadcast([P, P, 2, 2]),
                    op=MULT,
                )

        def quant(i):
            codes = work.tile([P, 2 * P], U32, tag="codes", name="codes", align_bytes=64)
            scales = work.tile([P, 2 * P], U8, tag="scales", name="scales", align_bytes=64)
            nc.vector.quantize_mx(out=codes[:].bitcast(FP8X4), scales=scales[:], in_=st["grp", i][:].rearrange("p o r j -> p (o r j)"))
            st["q", i] = (codes, scales)

        def mm_z(i, h):
            codes, scales = st["q", i]
            bank = psum.tile([P, D], F32, tag="bank", name="zb", bufs=8)
            for o, (w, sc) in enumerate(((wm, wm_sc), (ws, ws_sc))):
                nc.tensor.matmul_mx(
                    out=bank[:],
                    lhsT=codes[:, o * P : (o + 1) * P].bitcast(FP8X4),
                    lhsT_scale=scales[:, o * P : (o + 1) * P],
                    rhs=w[:, 2 * D * h : 2 * D * (h + 1)].bitcast(FP4X4),
                    rhs_scale=sc[:, D * h : D * (h + 1)],
                    start=(o == 0),
                    stop=(o == 1),
                )
            st["z", h, i] = bank

        def act(i, h):
            name, func = (("sg", ACT.Sigmoid), ("th", ACT.Tanh))[h]
            r = work.tile([P, 4, P], F32, tag=name, name=name, align_bytes=64)
            nc.scalar.activation(out=r[:], in_=st["z", h, i][:].rearrange("p (m t) -> p t m", t=4), func=func)
            st[name, i] = r

        def uprod(i):
            u = work.tile([P, 4, P], F32, tag="u", name="u", align_bytes=64)
            nc.vector.tensor_tensor(out=u[:], in0=st["sg", i][:], in1=st["th", i][:], op=MULT)
            st["u", i] = u

        def turn_u(i):
            bank = psum.tile([P, 4, P], F32, tag="bank", name="ut", bufs=8)
            for t in range(4):
                nc.tensor.transpose(bank[:, t, :], st["u", i][:, t, :], ident[:])
            st["ut", i] = bank

        def gain(i):
            ug = work.tile([P, P, 4], BF16, tag="ug", name="ug", align_bytes=64)
            nc.vector.tensor_tensor(
                out=ug[:],
                in0=st["ut", i][:].rearrange("p t r -> p r t"),
                in1=g_part[:].unsqueeze(1).to_broadcast([P, P, 4]),
                op=MULT,
            )
            st["ug", i] = ug

        def quant_u(i):
            codes = work.tile([P, P], U32, tag="ucodes", name="ucodes", bufs=6, align_bytes=64)
            scales = work.tile([P, P], U8, tag="uscales", name="uscales", bufs=6, align_bytes=64)
            nc.vector.quantize_mx(out=codes[:].bitcast(FP8X4), scales=scales[:], in_=st["ug", i][:].rearrange("p r t -> p (r t)"))
            st["uq", i] = (codes, scales)

        def mm_o(i, h):
            codes, scales = st["uq", i]
            bank = psum.tile([P, D], F32, tag="bank", name="ob", bufs=8)
            nc.tensor.matmul_mx(
                out=bank[:],
                lhsT=codes[:].bitcast(FP8X4),
                lhsT_scale=scales[:],
                rhs=wo[:, 2 * D * h : 2 * D * (h + 1)].bitcast(FP4X4),
                rhs_scale=wo_sc[:, D * h : D * (h + 1)],
                start=True,
                stop=True,
            )
            st["o", h, i] = bank

        def scale_x(i):
            nc.scalar.activation(out=xs_sb[:, i, :], in_=x_sb[:, i, :], func=ACT.Copy, scale=RSQRT2)

        def skip(i):
            r = work.tile([P, D], F32, tag="sk", name="sk", align_bytes=64)
            nc.scalar.copy(out=r[:], in_=st["o", 1, i][:])
            nc.sync.dma_start(out=skip_v[:, i, :], in_=r[:])

        def xnew(i):
            r = work.tile([P, D], F32, tag="xn", name="xn", align_bytes=64)
            nc.vector.scalar_tensor_tensor(out=r[:], in0=st["o", 0, i][:], scalar=RSQRT2, in1=xs_sb[:, i, :], op0=MULT, op1=ADD)
            nc.sync.dma_start(out=xnew_v[:, i, :], in_=r[:])

        warm_up(3)
        spread_scales()
        warm_up(1)
        yprod(0)
        yprod(1)
        turn(0)
        yprod(2)
        turn(1)
        evac(0)
        evac_y(0)
        turn(2)
        warm_up(2)
        yprod(3)
        quant(0)
        evac(1)
        evac_y(1)
        done = {(yprod, 0), (yprod, 1), (yprod, 2), (yprod, 3), (turn, 0), (turn, 1), (turn, 2), (evac, 0), (evac, 1), (quant, 0)}
        order = (
            (mm_z, -1, 1),
            (mm_z, -1, 0),
            (quant, -2),
            (turn, -4),
            (skip, 4),
            (turn_u, 1),
            (turn, -5),
            (xnew, 4),
            (uprod, 0),
            (quant_u, 2),
            (quant, -3),
            (act, -1, 1),
            (turn_u, 0),
            (mm_z, -2, 0),
            (act, -1, 0),
            (evac, -4),
            (scale_x, 0),
            (evac, -5),
            (yprod, -7),
            (xnew, 3),
            (gain, 1),
            (gain, 0),
            (mm_z, -2, 1),
            (quant_u, 1),
            (act, -2, 0),
            (mm_o, 3, 1),
            (act, -2, 1),
            (mm_o, 2, 0),
            (skip, 3),
            (uprod, -1),
            (mm_o, 2, 1),
            (scale_x, 1),
            (yprod, -6),
            (mm_o, 1, 0),
        )
        for s in range(-5, 8):
            for stage, lag, *args in order:
                i = 2 * s - lag
                if 0 <= i < TILES and (stage, i) not in done:
                    stage(i, *args)
